import numpy as np
import ml_dtypes


def mxq(x, axis, fmt="e4m3"):
    dtype, down = {"e4m3": (ml_dtypes.float8_e4m3fn, 7), "e5m2": (ml_dtypes.float8_e5m2, 14)}[fmt]
    v = np.moveaxis(np.asarray(x, np.float32).astype(ml_dtypes.bfloat16).astype(np.float64), axis, -1)
    blocks = v.reshape(v.shape[:-1] + (-1, 32))
    amax = np.abs(blocks).max(-1, keepdims=True)
    byte = np.maximum(np.where(amax > 0, np.frexp(amax)[1] - 1 + 127, 0) - down, 1)
    scale = np.exp2(byte - 127.0)
    codes = (blocks / scale).astype(np.float32).astype(dtype).astype(np.float64)
    return np.moveaxis((codes * scale).reshape(v.shape), -1, axis)


WIDE = False


def mx_kscale(k):
    if not WIDE:
        return np.ones(k)
    levels = np.array([10, -10, 5, -5, 0])
    if k % 512:
        return np.exp2(np.random.permutation(np.resize(levels, k // 32))).repeat(32)
    a = np.empty((k // 512, 16))
    for p in range(k // 512):
        a[p, :8] = np.random.permutation(np.resize(levels, 8))
        for g in range(8):
            far = levels[np.abs(levels - a[p, g]) >= 10]
            a[p, g + 8] = far[np.random.randint(len(far))]
    return np.exp2(a.ravel()).repeat(32)


BF16 = ml_dtypes.bfloat16


def bf(x):
    return np.asarray(x, np.float32).astype(BF16)


def f64(x):
    return np.asarray(x).astype(np.float64)


E2M1 = np.array([0.0, 0.5, 1.0, 1.5, 2.0, 3.0, 4.0, 6.0, -0.0, -0.5, -1.0, -1.5, -2.0, -3.0, -4.0, -6.0])


def pack_weight(w, fmt):
    k, n = w.shape
    w = f64(bf(w)).reshape(k // 32, 32, n)
    amax = np.abs(w).max(1)
    if fmt == "e4m3":
        byte = np.frexp(amax)[1] - 1 + 127 - 7
    else:
        mant, ex = np.frexp(amax / 6.0)
        byte = np.where(mant > 0.5, ex, ex - 1) + 127
    byte = np.clip(np.where(amax > 0, byte, 1), 1, 254)
    scaled = (w * np.exp2(127.0 - byte)[:, None, :]).reshape(k, n).astype(np.float32)
    by_word = np.ascontiguousarray(scaled.reshape(k // 512, 128, 4, n).transpose(0, 1, 3, 2))
    if fmt == "e4m3":
        words = by_word.astype(ml_dtypes.float8_e4m3fn).view(np.uint8)
    else:
        c = by_word.astype(ml_dtypes.float4_e2m1fn).view(np.uint8) & 0xF
        words = c[..., 0::2] | (c[..., 1::2] << 4)
    return np.ascontiguousarray(words), np.ascontiguousarray(byte.astype(np.uint8).reshape(k // 512, 16, n))


def unpack_weight(words, scales, fmt):
    g, p, n, _ = words.shape
    if fmt == "e4m3":
        vals = np.ascontiguousarray(words).view(ml_dtypes.float8_e4m3fn).astype(np.float64)
    else:
        nib = np.empty((g, p, n, 4), np.uint8)
        nib[..., 0::2] = words & 0xF
        nib[..., 1::2] = words >> 4
        vals = E2M1[nib]
    vals = vals * np.repeat(np.exp2(scales.astype(np.float64) - 127.0), 8, axis=1)[..., None]
    return vals.transpose(0, 1, 3, 2).reshape(g * 512, n)
def pack4(w):
    words, scales = pack_weight(w, "e2m1")
    return words.reshape(words.shape[0], 128, -1), scales


def unpack4(words, scales):
    return unpack_weight(words.reshape(words.shape[0], 128, -1, 2), scales, "e2m1")


C, N, D, F, O = 3, 256, 512, 1024, 512


def draw0():
    s, t = mx_kscale(D), mx_kscale(F)
    x = bf(np.random.standard_normal((C, N, D)) * s)
    w_words, w_scales = pack4(np.random.standard_normal((D, F)) / np.sqrt(D) / s[:, None])
    u_words, u_scales = pack4(np.random.standard_normal((D, F)) * 0.05 / np.sqrt(D) / s[:, None])
    g = bf((1.0 + 0.1 * np.random.standard_normal(F)) * t)
    v_words, v_scales = pack4(np.random.standard_normal((F, O)) / np.sqrt(F) / t[:, None])
    return {"x": x, "w_words": w_words, "w_scales": w_scales, "u_words": u_words, "u_scales": u_scales, "g": g, "v_words": v_words, "v_scales": v_scales}


def spatial_dot(a, b):
    return np.sum(a * b, axis=0)


def core(x, w_words, w_scales, u_words, u_scales, g, v_words, v_scales):
    xq = mxq(f64(x), 2, "e4m3")
    q = xq @ unpack4(w_words, w_scales)
    k = xq @ unpack4(u_words, u_scales)
    s = spatial_dot(q, k)
    kk = spatial_dot(k, k)
    r = 0.8 * np.minimum(s, 0.0) / (kk + 1e-4)
    h = (q - r[None, :, :] * k) * f64(g)[None, None, :]
    return mxq(h, 2, "e4m3") @ unpack4(v_words, v_scales)


def e4m3fn_bytes(y):
    return np.clip(np.asarray(y, np.float64), -448.0, 448.0).astype(np.float32).astype(ml_dtypes.float8_e4m3fn).view(np.uint8)


def e4m3fn_values(b):
    return np.asarray(b, np.uint8).view(ml_dtypes.float8_e4m3fn).astype(np.float64)


def setup_inputs():
    d = draw0()
    x0 = np.asarray(d['x']).astype(np.float64)
    s = (np.max(np.abs(x0), axis=(0, 1), keepdims=True) / 448.0).astype(np.float32)
    out = {}
    for k, v in d.items():
        if k == 'x':
            out['x_bytes'] = e4m3fn_bytes(x0 / s.astype(np.float64))
            out['x_scale'] = s
        else:
            out[k] = v
    return out


def reference(x_bytes, x_scale, w_words, w_scales, u_words, u_scales, g, v_words, v_scales):
    return core(e4m3fn_values(x_bytes) * x_scale.astype(np.float64), w_words, w_scales, u_words, u_scales, g, v_words, v_scales)

@@ -1,0 +1,384 @@
+from contextlib import ExitStack
+
+import concourse.mybir as mybir
+from concourse.masks import make_identity
+
+F32 = mybir.dt.float32
+BF16 = mybir.dt.bfloat16
+I32 = mybir.dt.int32
+U32 = mybir.dt.uint32
+U8 = mybir.dt.uint8
+FP8 = mybir.dt.float8_e4m3fn
+FP8X4 = mybir.dt.float8_e4m3fn_x4
+FP4X4 = mybir.dt.float4_e2m1fn_x4
+ALU = mybir.AluOpType
+ACT = mybir.ActivationFunctionType
+
+C, N, D, F, O = 3, 256, 512, 1024, 512
+P = 128
+PACK = 4
+KP = P * PACK
+NT = N // P
+NG = F // KP
+SLOPE = 0.8
+EPS = 1e-4
+MANUAL = True
+KB = 10
+WARM = False
+WENG = "vsv"
+POOL = [0, 1, 1, 1]
+OD = True
+SMODE = "MMMM"
+KENG = "s" * 12
+QENG = "s" * 12
+SQENG = "s" * 12
+PENG = "p" * 12
+OENG = "sssssv"
+BMX, BMID, BD = 5, 1, 2
+PM = [
+    ("rr", 0, 2), ("kc", -1, 0), ("mq", -1, 0), ("mq", -1, 1), ("mq", -1, 2), ("qz", 1, 2), ("tt", 0, 0), ("sq", -1, 1), ("tkk", -1, 0),
+    ("tt", 0, 1), ("kc", -1, 1), ("tkk", -1, 1), ("td", 0, 0), ("tt", 0, 2), ("sq", -1, 2), ("pp", -1, 0), ("ss", -1, 0),
+    ("kc", -1, 2), ("tkk", -1, 2), ("td", 0, 1), ("pp", -1, 1), ("ss", -1, 1), ("qc", -1, 0), ("ev", 0, 0), ("rs", -1, 2), ("tq", 0, 2), ("td", 0, 2),
+    ("mk", -2, 0), ("mk", -2, 1), ("mk", -2, 2), ("mo", 1, 0), ("pp", -1, 2), ("qc", -1, 1), ("ev", 0, 1), ("yy", -1, 2), ("ty", -1, 2), ("mo", 1, 1), ("mo", 1, 2),
+    ("ev", 0, 2), ("qc", -1, 2), ("ss", -1, 2), ("tq", -1, 0), ("tq", -1, 1), ("qz", 0, 0), ("qz", 0, 1),
+    ("sq", -2, 0), ("oc", 1, 0), ("oc", 1, 1), ("oc", 1, 2),
+]
+HEAD = [("x1", 0), ("mk", 0), ("mk", 1), ("mk", 2), ("mq", 0), ("x1", 1), ("x1", 2), ("sq", 0), ("sq", 1), ("sq", 2),
+        ("tkk", 0), ("tkk", 1), ("tkk", 2), ("kc", 0), ("mq", 1), ("mq", 2), ("kc", 1), ("pp", 0), ("ss", 0), ("rs", 2), ("pp", 1), ("kc", 2), ("x1q", 0), ("ss", 1),
+        ("yy", 2), ("pp", 2), ("x1q", 1), ("mk", 3), ("mk", 4), ("ty", 2), ("qc", 0), ("qc", 1), ("ss", 2), ("x1q", 2), ("mk", 5), ("qc", 2), ("tq", 0), ("tq", 1), ("sq", 3)]
+TAIL = [("rr", 11), ("qz", 8), ("tt", 9), ("tt", 10), ("td", 9), ("tq", 11), ("tt", 11), ("td", 10), ("ev", 9),
+    ("td", 11), ("m1", 9), ("m1", 10), ("m1", 11), ("ev", 10), ("qz", 9), ("m2", 9), ("ev", 11), ("qz", 10), ("oc", 9), ("m2", 10), ("qz", 11), ("m2", 11), ("oc", 10), ("oc", 11)]
+PERIOD = PM
+FLOPS = 2 * C * N * D * F * 2 + 2 * C * N * F * O
+
+
+def tile_vectorneurondirectionalleaky_w4_kernel(
+    tc, x_bytes, x_scale, w_words, w_scales, u_words, u_scales, g, v_words, v_scales, out
+):
+    nc = tc.nc
+    with ExitStack() as ctx:
+        keep = ctx.enter_context(tc.tile_pool(name="keep", bufs=1))
+        work = ctx.enter_context(tc.tile_pool(name="work", bufs=6))
+        mid = ctx.enter_context(tc.tile_pool(name="mid", bufs=2))
+        ps_mx = ctx.enter_context(tc.psum_pool(name="ps_mx", bufs=BMX))
+        ps_mid = ctx.enter_context(tc.psum_pool(name="ps_mid", bufs=BMID))
+        ps_d = ctx.enter_context(tc.psum_pool(name="ps_d", bufs=BD))
+
+
+        us = keep.tile([P, F], U8, name="us", align_bytes=64)
+        ws = keep.tile([P, F], U8, name="ws", align_bytes=64)
+        vs = keep.tile([P, NG * O], U8, name="vs", align_bytes=64)
+        if WARM:
+            warm = keep.tile([P, 8], F32, name="warm")
+        nc.vector.memset(us[:].bitcast(I32), 0)
+        nc.vector.memset(ws[:].bitcast(I32), 0)
+        if WARM:
+            nc.vector.memset(warm[:, 0:1], 1.0)
+        nc.vector.memset(vs[:].bitcast(I32), 0)
+        if WARM:
+            nc.scalar.activation(out=warm[:, 4:5], in_=warm[:, 0:1], func=ACT.Abs_reciprocal_sqrt)
+            zeros = keep.tile([P, KP], BF16, name="zeros")
+            nc.gpsimd.memset(zeros[:], 0.0)
+            idle = ps_mid.tile([P, KP], F32, name="bank_mid")
+
+        def spin(n):
+            if WARM:
+                for a in range(n):
+                    nc.tensor.matmul(idle[:], lhsT=zeros[:, 0:P], rhs=zeros[:], start=True, stop=True)
+
+        ident = keep.tile([P, P], F32, name="ident")
+        make_identity(nc, ident[:])
+
+        def load_scales(dst, src):
+            for q in range(4):
+                nc.sync.dma_start(
+                    out=dst[32 * q : 32 * q + 4, :].bitcast(I32), in_=src[4 * q : 4 * q + 4, :].bitcast(I32)
+                )
+
+        def load_words(name, src, gi):
+            t = keep.tile([P, 2 * KP], U8, name=name, align_bytes=64)
+            nc.sync.dma_start(out=t[:].bitcast(I32), in_=src[0, :, 2 * KP * gi : 2 * KP * (gi + 1)].bitcast(I32))
+            return t
+
+        def load_x(j):
+            t = keep.tile([P, C, D], U8, name="xb%d" % j, align_bytes=64)
+            nc.sync.dma_start(out=t[:], in_=x_bytes[:, j * P : (j + 1) * P, :].rearrange("c n k -> n c k"))
+            return t
+
+        xb = {}
+        uw = {}
+        ww = {}
+        xb[0] = load_x(0)
+        xs = keep.tile([P, PACK], F32, name="xs")
+        nc.sync.dma_start(out=xs[:], in_=x_scale.rearrange("a b (p t) -> p (a b t)", t=PACK))
+        uw[0] = load_words("uw0", u_words, 0)
+        load_scales(us, u_scales[0])
+        xb[1] = load_x(1)
+        ww[0] = load_words("ww0", w_words, 0)
+        load_scales(ws, w_scales[0])
+        uw[1] = load_words("uw1", u_words, 1)
+        ww[1] = load_words("ww1", w_words, 1)
+        gain = keep.tile([P, NG, PACK], BF16, name="gain")
+        nc.sync.dma_start(out=gain[:], in_=g.rearrange("(a p t) -> p a t", p=P, t=PACK))
+        vw = keep.tile([P, NG, 2 * O], U8, name="vw", align_bytes=64)
+        nc.sync.dma_start(out=vw[:].bitcast(I32), in_=v_words.rearrange("a p b -> p a b").bitcast(I32))
+        for q in range(4):
+            nc.sync.dma_start(
+                out=vs[32 * q : 32 * q + 4, :].bitcast(I32).rearrange("r (a n) -> r a n", a=NG),
+                in_=v_scales[:, 4 * q : 4 * q + 4, :].bitcast(I32).rearrange("a r n -> r a n"),
+            )
+
+        xq = {}
+
+        wide = {}
+        xg = {}
+
+        def widen(j, c, eng):
+            t = work.tile([P, D], BF16, name="wide", align_bytes=64)
+            copy_on(eng, t[:], xb[j][:, c, :].bitcast(FP8))
+            wide[(j, c)] = t
+
+        def turn_x(j, c):
+            words = wide[(j, c)][:].bitcast(F32)
+            xt = ps_mx.tile([P, KP], F32, name="bank_mx") if j == 0 else ps_d.tile([P, KP], F32, name="bank_d")
+            for u in range(2):
+                nc.tensor.transpose(xt[:, u * P : (u + 1) * P], words[:, u : D // 2 : 2], ident[:])
+            t = work.tile([P, D], BF16, name="xg", align_bytes=64)
+            nc.vector.tensor_tensor(
+                out=t[:].rearrange("p (n u e) -> p n u e", u=2, e=2),
+                in0=xt[:, 0 : 2 * P].bitcast(BF16).rearrange("p (u n e) -> p n u e", u=2, e=2),
+                in1=xs[:].rearrange("p (u e) -> p u e", u=2).unsqueeze(1).to_broadcast([P, P, 2, 2]),
+                op=ALU.mult,
+            )
+            xg[(j, c)] = t
+
+        def quant_x(j, c):
+            codes = keep.tile([P, P], U32, name="xc%d%d" % (j, c), align_bytes=64)
+            plane = keep.tile([P, P], U8, name="xp%d%d" % (j, c), align_bytes=64)
+            nc.vector.quantize_mx(out=codes[:].bitcast(FP8X4), scales=plane[:], in_=xg[(j, c)][:])
+            xq[(j, c)] = (codes, plane)
+
+        st = {}
+
+        def perm(ap):
+            return ap.rearrange("n (m t) -> n t m", t=PACK)
+
+        def flat(ap):
+            return ap.rearrange("n (t m) -> n t m", t=PACK)
+
+        def turn(bank, src, start, stop):
+            for t in range(PACK):
+                cols = slice(t * P, (t + 1) * P)
+                nc.tensor.matmul(
+                    bank[:, cols], lhsT=src[:, cols], rhs=ident[:], is_transpose=True,
+                    start=(start and t == 0), stop=(stop and t == PACK - 1),
+                )
+
+        def copy_on(eng, out, in_):
+            if eng == "v":
+                nc.vector.tensor_copy(out=out, in_=in_)
+            else:
+                nc.scalar.copy(out=out, in_=in_)
+
+        def mx_pass(i, words, planes):
+            j, gi, c = slot(i)
+            codes, plane = xq[(j, c)]
+            bank = ps_mx.tile([P, KP], F32, name="bank_mx")
+            nc.tensor.matmul_mx(out=bank[:], lhsT=codes[:].bitcast(FP8X4), lhsT_scale=plane[:],
+                                rhs=words[gi][:].bitcast(FP4X4), rhs_scale=planes[:, gi * KP : (gi + 1) * KP],
+                                start=True, stop=True)
+            return bank
+
+        def slot(i):
+            return i // (NG * C), (i // C) % NG, i % C
+
+        def mk(i):
+            st[(i, "kb")] = mx_pass(i, uw, us)
+
+        def mq(i):
+            st[(i, "qb")] = mx_pass(i, ww, ws)
+
+        def kc(i):
+            k_sb = work.tile([P, KP], F32, name="k_sb", bufs=KB)
+            copy_on(KENG[i], flat(k_sb[:]), perm(st[(i, "kb")][:]))
+            st[(i, "k")] = k_sb
+
+        def sq(i):
+            t = work.tile([P, KP], F32, name="sq", bufs=3)
+            if SQENG[i] == "s":
+                nc.scalar.activation(out=flat(t[:]), in_=perm(st[(i, "kb")][:]), func=ACT.Square,
+                                     scale=(1.0 / SLOPE) ** 0.5)
+            elif SQENG[i] == "v":
+                nc.vector.tensor_tensor(out=t[:], in0=st[(i, "k")][:], in1=st[(i, "k")][:], op=ALU.mult)
+            else:
+                nc.gpsimd.tensor_tensor(out=t[:], in0=st[(i, "k")][:], in1=st[(i, "k")][:], op=ALU.mult)
+            st[(i, "sq")] = t
+
+        def qc(i):
+            q_sb = work.tile([P, KP], F32, name="q_sb", bufs=KB)
+            copy_on(QENG[i], flat(q_sb[:]), perm(st[(i, "qb")][:]))
+            st[(i, "q")] = q_sb
+
+        def pp(i):
+            pr = work.tile([P, KP], F32, name="pr", bufs=4)
+            if PENG[i] == "p":
+                nc.vector.tensor_tensor(out=flat(pr[:]), in0=perm(st[(i, "qb")][:]), in1=flat(st[(i, "k")][:]),
+                                        op=ALU.mult)
+            elif PENG[i] == "v":
+                nc.vector.tensor_tensor(out=pr[:], in0=st[(i, "q")][:], in1=st[(i, "k")][:], op=ALU.mult)
+            else:
+                nc.gpsimd.tensor_tensor(out=pr[:], in0=st[(i, "q")][:], in1=st[(i, "k")][:], op=ALU.mult)
+            st[(i, "p")] = pr
+
+        def tkk(i):
+            u, c = divmod(i, C)
+            if c == 0:
+                st[(u, "kkb")] = ps_mid.tile([P, KP], F32, name="bank_mid")
+            turn(st[(u, "kkb")], st[(i, "sq")], c == 0, c == C - 1)
+
+        def ss(i):
+            u, c = divmod(i, C)
+            if SMODE[u] == "F":
+                if c == 0:
+                    st[(u, "s")] = ps_mid.tile([P, KP], F32, name="bank_mid")
+                turn(st[(u, "s")], st[(i, "p")], c == 0, c == C - 1)
+            elif c == 0:
+                st[(u, "s")] = st[(i, "p")]
+            else:
+                s = mid.tile([P, KP], F32, name="s%d" % c)
+                eng = nc.gpsimd if (c == 1 and POOL[u]) else nc.vector
+                eng.tensor_tensor(out=s[:], in0=st[(u, "s")][:], in1=st[(i, "p")][:], op=ALU.add)
+                st[(u, "s")] = s
+
+        def rs(i):
+            u, c = divmod(i, C)
+            if c == C - 1:
+                t = mid.tile([P, KP], F32, name="rs")
+                nc.scalar.activation(out=t[:], in_=st[(u, "kkb")][:], func=ACT.Abs_reciprocal_sqrt,
+                                     bias=EPS / SLOPE)
+                st[(u, "rs")] = t
+
+        def yy(i):
+            u, c = divmod(i, C)
+            if c == C - 1:
+                y = mid.tile([P, KP], F32, name="y")
+                nc.scalar.activation(out=y[:], in_=st[(u, "rs")][:], func=ACT.Square)
+                st[(u, "y")] = y
+
+        def ty(i):
+            u, c = divmod(i, C)
+            if c == C - 1 and SMODE[u] == "M":
+                yb = ps_mid.tile([P, KP], F32, name="bank_mid")
+                turn(yb, st[(u, "y")], True, True)
+                st[(u, "y")] = yb
+
+        def rr(i):
+            u, c = divmod(i, C)
+            if c == C - 1:
+                r = mid.tile([P, KP], F32, name="r")
+                nc.vector.scalar_tensor_tensor(out=r[:], in0=st[(u, "s")][:], scalar=0.0, in1=st[(u, "y")][:],
+                                               op0=ALU.min, op1=ALU.mult)
+                st[(u, "r")] = r
+
+        def tr(i):
+            u, c = divmod(i, C)
+            if c == C - 1 and SMODE[u] == "F":
+                rb = ps_mid.tile([P, KP], F32, name="bank_mid")
+                turn(rb, st[(u, "r")], True, True)
+                st[(u, "r")] = rb
+
+        def tt(i):
+            tk = work.tile([P, KP], F32, name="tk", bufs=3)
+            nc.vector.scalar_tensor_tensor(out=tk[:], in0=st[(i, "k")][:], scalar=-1.0, in1=st[(i // C, "r")][:],
+                                           op0=ALU.mult, op1=ALU.mult)
+            st[(i, "t")] = tk
+
+        def tq(i):
+            db = ps_mx.tile([P, KP], F32, name="bank_mx") if i == 11 else ps_d.tile([P, KP], F32, name="bank_d")
+            turn(db, st[(i, "q")], True, False)
+            st[(i, "d")] = db
+
+        def td(i):
+            turn(st[(i, "d")], st[(i, "t")], False, True)
+
+        def ev(i):
+            j, gi, c = slot(i)
+            h = work.tile([P, KP], BF16, name="h", bufs=3, align_bytes=64)
+            nc.vector.tensor_tensor(
+                out=h[:].rearrange("p (n t) -> p n t", t=PACK),
+                in0=st[(i, "d")][:].rearrange("p (t n) -> p n t", t=PACK),
+                in1=gain[:, gi, :].unsqueeze(1).to_broadcast([P, P, PACK]),
+                op=ALU.mult,
+            )
+            st[(i, "h")] = h
+
+        def qz(i):
+            codes = work.tile([P, P], U32, name="hc", bufs=12, align_bytes=64)
+            plane = work.tile([P, P], U8, name="hp", bufs=12, align_bytes=64)
+            nc.vector.quantize_mx(out=codes[:].bitcast(FP8X4), scales=plane[:], in_=st[(i, "h")][:])
+            st[(i, "hq")] = (codes, plane)
+
+        def mo(i):
+            j, gi, c = slot(i)
+            if gi == NG - 1:
+                ob = ps_mx.tile([P, O], F32, name="bank_mx")
+                for a in range(NG):
+                    codes, plane = st[(i - C * (NG - 1 - a), "hq")]
+                    nc.tensor.matmul_mx(out=ob[:], lhsT=codes[:].bitcast(FP8X4), lhsT_scale=plane[:],
+                                        rhs=vw[:, a, :].bitcast(FP4X4), rhs_scale=vs[:, a * O : (a + 1) * O],
+                                        start=(a == 0), stop=(a == NG - 1))
+                st[(i, "ob")] = ob
+
+        def mpass(i, a):
+            codes, plane = st[(i - C * (NG - 1 - a), "hq")]
+            nc.tensor.matmul_mx(out=st[(i, "ob")][:], lhsT=codes[:].bitcast(FP8X4), lhsT_scale=plane[:],
+                                rhs=vw[:, a, :].bitcast(FP4X4), rhs_scale=vs[:, a * O : (a + 1) * O],
+                                start=(a == 0), stop=(a == NG - 1))
+
+        def m1(i):
+            st[(i, "ob")] = ps_mx.tile([P, O], F32, name="bank_mx")
+            mpass(i, 0)
+
+        def m2(i):
+            mpass(i, 1)
+
+        def oc(i):
+            j, gi, c = slot(i)
+            if gi == NG - 1:
+                res = work.tile([P, O], F32, name="res", bufs=3)
+                copy_on(OENG[j * C + c], res[:], st[(i, "ob")][:])
+                nc.sync.dma_start(out=out[c, j * P : (j + 1) * P, :], in_=res[:])
+
+        def x1(i):
+            if i < C:
+                turn_x(1, i)
+
+        def x1q(i):
+            if i < C:
+                quant_x(1, i)
+
+        stages = dict(mk=mk, mq=mq, kc=kc, sq=sq, qc=qc, pp=pp, tkk=tkk, ss=ss, rs=rs, yy=yy, ty=ty, rr=rr, tr=tr,
+                      tt=tt, tq=tq, td=td, ev=ev, qz=qz, mo=mo, oc=oc, x1=x1, x1q=x1q, m1=m1, m2=m2)
+        with ExitStack() as sched:
+            if MANUAL:
+                sched.enter_context(tc.manual_schedule())
+            spin(5)
+            for c in range(C):
+                widen(0, c, WENG[c])
+            for c in range(C):
+                widen(1, c, "s")
+            for c in range(C):
+                turn_x(0, c)
+                if c > 0:
+                    quant_x(0, c - 1)
+            quant_x(0, C - 1)
+            spin(1)
+            units = NT * NG
+            for name, c in HEAD:
+                stages[name](c)
+            for u in range(units - 1):
+                for name, du, c in PERIOD:
+                    if 0 <= u - du < units:
+                        stages[name](C * (u - du) + c)
+            for name, i in TAIL:
+                stages[name](i)

@@ -18,37 +18,14 @@ C, N, D, F, O = 3, 256, 512, 1024, 512
 P = 128
 PACK = 4
 KP = P * PACK
-NT = N // P
-NG = F // KP
+HALVES = F // KP
+UNITS = (N // P) * HALVES
+LAST = UNITS - 1
 SLOPE = 0.8
 EPS = 1e-4
-MANUAL = True
-KB = 10
-WARM = False
-WENG = "vsv"
-POOL = [0, 1, 1, 1]
-OD = True
-SMODE = "MMMM"
-KENG = "s" * 12
-QENG = "s" * 12
-SQENG = "s" * 12
-PENG = "p" * 12
-OENG = "sssssv"
-BMX, BMID, BD = 5, 1, 2
-PM = [
-    ("rr", 0, 2), ("kc", -1, 0), ("mq", -1, 0), ("mq", -1, 1), ("mq", -1, 2), ("qz", 1, 2), ("tt", 0, 0), ("sq", -1, 1), ("tkk", -1, 0),
-    ("tt", 0, 1), ("kc", -1, 1), ("tkk", -1, 1), ("td", 0, 0), ("tt", 0, 2), ("sq", -1, 2), ("pp", -1, 0), ("ss", -1, 0),
-    ("kc", -1, 2), ("tkk", -1, 2), ("td", 0, 1), ("pp", -1, 1), ("ss", -1, 1), ("qc", -1, 0), ("ev", 0, 0), ("rs", -1, 2), ("tq", 0, 2), ("td", 0, 2),
-    ("mk", -2, 0), ("mk", -2, 1), ("mk", -2, 2), ("mo", 1, 0), ("pp", -1, 2), ("qc", -1, 1), ("ev", 0, 1), ("yy", -1, 2), ("ty", -1, 2), ("mo", 1, 1), ("mo", 1, 2),
-    ("ev", 0, 2), ("qc", -1, 2), ("ss", -1, 2), ("tq", -1, 0), ("tq", -1, 1), ("qz", 0, 0), ("qz", 0, 1),
-    ("sq", -2, 0), ("oc", 1, 0), ("oc", 1, 1), ("oc", 1, 2),
-]
-HEAD = [("x1", 0), ("mk", 0), ("mk", 1), ("mk", 2), ("mq", 0), ("x1", 1), ("x1", 2), ("sq", 0), ("sq", 1), ("sq", 2),
-        ("tkk", 0), ("tkk", 1), ("tkk", 2), ("kc", 0), ("mq", 1), ("mq", 2), ("kc", 1), ("pp", 0), ("ss", 0), ("rs", 2), ("pp", 1), ("kc", 2), ("x1q", 0), ("ss", 1),
-        ("yy", 2), ("pp", 2), ("x1q", 1), ("mk", 3), ("mk", 4), ("ty", 2), ("qc", 0), ("qc", 1), ("ss", 2), ("x1q", 2), ("mk", 5), ("qc", 2), ("tq", 0), ("tq", 1), ("sq", 3)]
-TAIL = [("rr", 11), ("qz", 8), ("tt", 9), ("tt", 10), ("td", 9), ("tq", 11), ("tt", 11), ("td", 10), ("ev", 9),
-    ("td", 11), ("m1", 9), ("m1", 10), ("m1", 11), ("ev", 10), ("qz", 9), ("m2", 9), ("ev", 11), ("qz", 10), ("oc", 9), ("m2", 10), ("qz", 11), ("m2", 11), ("oc", 10), ("oc", 11)]
-PERIOD = PM
+
+BANKS_MX, BANKS_KK, BANKS_DIFF = 5, 1, 2
+
 FLOPS = 2 * C * N * D * F * 2 + 2 * C * N * F * O
 
 
@@ -58,113 +35,80 @@ def tile_vectorneurondirectionalleaky_w4_kernel(
     nc = tc.nc
     with ExitStack() as ctx:
         keep = ctx.enter_context(tc.tile_pool(name="keep", bufs=1))
-        work = ctx.enter_context(tc.tile_pool(name="work", bufs=6))
+        work = ctx.enter_context(tc.tile_pool(name="work", bufs=2 * C))
         mid = ctx.enter_context(tc.tile_pool(name="mid", bufs=2))
-        ps_mx = ctx.enter_context(tc.psum_pool(name="ps_mx", bufs=BMX))
-        ps_mid = ctx.enter_context(tc.psum_pool(name="ps_mid", bufs=BMID))
-        ps_d = ctx.enter_context(tc.psum_pool(name="ps_d", bufs=BD))
+        ps_mx = ctx.enter_context(tc.psum_pool(name="ps_mx", bufs=BANKS_MX))
+        ps_kk = ctx.enter_context(tc.psum_pool(name="ps_kk", bufs=BANKS_KK))
+        ps_diff = ctx.enter_context(tc.psum_pool(name="ps_diff", bufs=BANKS_DIFF))
 
-
-        us = keep.tile([P, F], U8, name="us", align_bytes=64)
-        ws = keep.tile([P, F], U8, name="ws", align_bytes=64)
-        vs = keep.tile([P, NG * O], U8, name="vs", align_bytes=64)
-        if WARM:
-            warm = keep.tile([P, 8], F32, name="warm")
-        nc.vector.memset(us[:].bitcast(I32), 0)
-        nc.vector.memset(ws[:].bitcast(I32), 0)
-        if WARM:
-            nc.vector.memset(warm[:, 0:1], 1.0)
-        nc.vector.memset(vs[:].bitcast(I32), 0)
-        if WARM:
-            nc.scalar.activation(out=warm[:, 4:5], in_=warm[:, 0:1], func=ACT.Abs_reciprocal_sqrt)
-            zeros = keep.tile([P, KP], BF16, name="zeros")
-            nc.gpsimd.memset(zeros[:], 0.0)
-            idle = ps_mid.tile([P, KP], F32, name="bank_mid")
-
-        def spin(n):
-            if WARM:
-                for a in range(n):
-                    nc.tensor.matmul(idle[:], lhsT=zeros[:, 0:P], rhs=zeros[:], start=True, stop=True)
+        u_plane = keep.tile([P, F], U8, name="u_plane", align_bytes=64)
+        w_plane = keep.tile([P, F], U8, name="w_plane", align_bytes=64)
+        v_plane = keep.tile([P, HALVES * O], U8, name="v_plane", align_bytes=64)
+        warm = keep.tile([P, 8], F32, name="warm")
+        nc.vector.memset(u_plane[:].bitcast(I32), 0)
+        nc.vector.memset(w_plane[:].bitcast(I32), 0)
+        nc.vector.memset(warm[:, 0:1], 1.0)
+        nc.vector.memset(v_plane[:].bitcast(I32), 0)
+        nc.scalar.activation(out=warm[:, 4:5], in_=warm[:, 0:1], func=ACT.Abs_reciprocal_sqrt)
 
         ident = keep.tile([P, P], F32, name="ident")
         make_identity(nc, ident[:])
 
-        def load_scales(dst, src):
-            for q in range(4):
+        def load_plane(plane, rows):
+            for quad in range(4):
                 nc.sync.dma_start(
-                    out=dst[32 * q : 32 * q + 4, :].bitcast(I32), in_=src[4 * q : 4 * q + 4, :].bitcast(I32)
+                    out=plane[32 * quad : 32 * quad + 4, :].bitcast(I32),
+                    in_=rows[4 * quad : 4 * quad + 4, :].bitcast(I32),
                 )
 
-        def load_words(name, src, gi):
-            t = keep.tile([P, 2 * KP], U8, name=name, align_bytes=64)
-            nc.sync.dma_start(out=t[:].bitcast(I32), in_=src[0, :, 2 * KP * gi : 2 * KP * (gi + 1)].bitcast(I32))
-            return t
+        def load_words(name, words, half):
+            tile = keep.tile([P, 2 * KP], U8, name=name, align_bytes=64)
+            nc.sync.dma_start(
+                out=tile[:].bitcast(I32), in_=words[0, :, 2 * KP * half : 2 * KP * (half + 1)].bitcast(I32)
+            )
+            return tile
 
         def load_x(j):
-            t = keep.tile([P, C, D], U8, name="xb%d" % j, align_bytes=64)
-            nc.sync.dma_start(out=t[:], in_=x_bytes[:, j * P : (j + 1) * P, :].rearrange("c n k -> n c k"))
-            return t
+            tile = keep.tile([P, C, D], U8, name="x_raw%d" % j, align_bytes=64)
+            nc.sync.dma_start(out=tile[:], in_=x_bytes[:, j * P : (j + 1) * P, :].rearrange("c n k -> n c k"))
+            return tile
 
-        xb = {}
-        uw = {}
-        ww = {}
-        xb[0] = load_x(0)
-        xs = keep.tile([P, PACK], F32, name="xs")
-        nc.sync.dma_start(out=xs[:], in_=x_scale.rearrange("a b (p t) -> p (a b t)", t=PACK))
-        uw[0] = load_words("uw0", u_words, 0)
-        load_scales(us, u_scales[0])
-        xb[1] = load_x(1)
-        ww[0] = load_words("ww0", w_words, 0)
-        load_scales(ws, w_scales[0])
-        uw[1] = load_words("uw1", u_words, 1)
-        ww[1] = load_words("ww1", w_words, 1)
-        gain = keep.tile([P, NG, PACK], BF16, name="gain")
+        x_raw = {}
+        u_tiles = {}
+        w_tiles = {}
+        x_raw[0] = load_x(0)
+        x_factor = keep.tile([P, PACK], F32, name="x_factor")
+        nc.sync.dma_start(out=x_factor[:], in_=x_scale.rearrange("a b (p t) -> p (a b t)", t=PACK))
+        u_tiles[0] = load_words("u_words0", u_words, 0)
+        load_plane(u_plane, u_scales[0])
+        x_raw[1] = load_x(1)
+        w_tiles[0] = load_words("w_words0", w_words, 0)
+        load_plane(w_plane, w_scales[0])
+        u_tiles[1] = load_words("u_words1", u_words, 1)
+        w_tiles[1] = load_words("w_words1", w_words, 1)
+        gain = keep.tile([P, HALVES, PACK], BF16, name="gain")
         nc.sync.dma_start(out=gain[:], in_=g.rearrange("(a p t) -> p a t", p=P, t=PACK))
-        vw = keep.tile([P, NG, 2 * O], U8, name="vw", align_bytes=64)
-        nc.sync.dma_start(out=vw[:].bitcast(I32), in_=v_words.rearrange("a p b -> p a b").bitcast(I32))
-        for q in range(4):
+        v_tile = keep.tile([P, HALVES, 2 * O], U8, name="v_tile", align_bytes=64)
+        nc.sync.dma_start(out=v_tile[:].bitcast(I32), in_=v_words.rearrange("a p b -> p a b").bitcast(I32))
+        for quad in range(4):
             nc.sync.dma_start(
-                out=vs[32 * q : 32 * q + 4, :].bitcast(I32).rearrange("r (a n) -> r a n", a=NG),
-                in_=v_scales[:, 4 * q : 4 * q + 4, :].bitcast(I32).rearrange("a r n -> r a n"),
+                out=v_plane[32 * quad : 32 * quad + 4, :].bitcast(I32).rearrange("r (a n) -> r a n", a=HALVES),
+                in_=v_scales[:, 4 * quad : 4 * quad + 4, :].bitcast(I32).rearrange("a r n -> r a n"),
             )
 
-        xq = {}
+        held = {}
 
-        wide = {}
-        xg = {}
+        def copy(on_vector, dst, src):
+            if on_vector:
+                nc.vector.tensor_copy(out=dst, in_=src)
+            else:
+                nc.scalar.copy(out=dst, in_=src)
 
-        def widen(j, c, eng):
-            t = work.tile([P, D], BF16, name="wide", align_bytes=64)
-            copy_on(eng, t[:], xb[j][:, c, :].bitcast(FP8))
-            wide[(j, c)] = t
+        def as_stored(bank):
+            return bank.rearrange("n (m t) -> n t m", t=PACK)
 
-        def turn_x(j, c):
-            words = wide[(j, c)][:].bitcast(F32)
-            xt = ps_mx.tile([P, KP], F32, name="bank_mx") if j == 0 else ps_d.tile([P, KP], F32, name="bank_d")
-            for u in range(2):
-                nc.tensor.transpose(xt[:, u * P : (u + 1) * P], words[:, u : D // 2 : 2], ident[:])
-            t = work.tile([P, D], BF16, name="xg", align_bytes=64)
-            nc.vector.tensor_tensor(
-                out=t[:].rearrange("p (n u e) -> p n u e", u=2, e=2),
-                in0=xt[:, 0 : 2 * P].bitcast(BF16).rearrange("p (u n e) -> p n u e", u=2, e=2),
-                in1=xs[:].rearrange("p (u e) -> p u e", u=2).unsqueeze(1).to_broadcast([P, P, 2, 2]),
-                op=ALU.mult,
-            )
-            xg[(j, c)] = t
-
-        def quant_x(j, c):
-            codes = keep.tile([P, P], U32, name="xc%d%d" % (j, c), align_bytes=64)
-            plane = keep.tile([P, P], U8, name="xp%d%d" % (j, c), align_bytes=64)
-            nc.vector.quantize_mx(out=codes[:].bitcast(FP8X4), scales=plane[:], in_=xg[(j, c)][:])
-            xq[(j, c)] = (codes, plane)
-
-        st = {}
-
-        def perm(ap):
-            return ap.rearrange("n (m t) -> n t m", t=PACK)
-
-        def flat(ap):
-            return ap.rearrange("n (t m) -> n t m", t=PACK)
+        def as_reordered(tile):
+            return tile.rearrange("n (t m) -> n t m", t=PACK)
 
         def turn(bank, src, start, stop):
             for t in range(PACK):
@@ -174,211 +118,318 @@ def tile_vectorneurondirectionalleaky_w4_kernel(
                     start=(start and t == 0), stop=(stop and t == PACK - 1),
                 )
 
-        def copy_on(eng, out, in_):
-            if eng == "v":
-                nc.vector.tensor_copy(out=out, in_=in_)
+
+        def widen_x(j, c, on_vector):
+            wide = work.tile([P, D], BF16, name="wide", align_bytes=64)
+            copy(on_vector, wide[:], x_raw[j][:, c, :].bitcast(FP8))
+            held["wide", j, c] = wide
+
+        def turn_x(j, c):
+            words = held["wide", j, c][:].bitcast(F32)
+            if j == 0:
+                bank = ps_mx.tile([P, KP], F32, name="bank_mx")
             else:
-                nc.scalar.copy(out=out, in_=in_)
-
-        def mx_pass(i, words, planes):
-            j, gi, c = slot(i)
-            codes, plane = xq[(j, c)]
-            bank = ps_mx.tile([P, KP], F32, name="bank_mx")
-            nc.tensor.matmul_mx(out=bank[:], lhsT=codes[:].bitcast(FP8X4), lhsT_scale=plane[:],
-                                rhs=words[gi][:].bitcast(FP4X4), rhs_scale=planes[:, gi * KP : (gi + 1) * KP],
-                                start=True, stop=True)
-            return bank
-
-        def slot(i):
-            return i // (NG * C), (i // C) % NG, i % C
-
-        def mk(i):
-            st[(i, "kb")] = mx_pass(i, uw, us)
-
-        def mq(i):
-            st[(i, "qb")] = mx_pass(i, ww, ws)
-
-        def kc(i):
-            k_sb = work.tile([P, KP], F32, name="k_sb", bufs=KB)
-            copy_on(KENG[i], flat(k_sb[:]), perm(st[(i, "kb")][:]))
-            st[(i, "k")] = k_sb
-
-        def sq(i):
-            t = work.tile([P, KP], F32, name="sq", bufs=3)
-            if SQENG[i] == "s":
-                nc.scalar.activation(out=flat(t[:]), in_=perm(st[(i, "kb")][:]), func=ACT.Square,
-                                     scale=(1.0 / SLOPE) ** 0.5)
-            elif SQENG[i] == "v":
-                nc.vector.tensor_tensor(out=t[:], in0=st[(i, "k")][:], in1=st[(i, "k")][:], op=ALU.mult)
-            else:
-                nc.gpsimd.tensor_tensor(out=t[:], in0=st[(i, "k")][:], in1=st[(i, "k")][:], op=ALU.mult)
-            st[(i, "sq")] = t
-
-        def qc(i):
-            q_sb = work.tile([P, KP], F32, name="q_sb", bufs=KB)
-            copy_on(QENG[i], flat(q_sb[:]), perm(st[(i, "qb")][:]))
-            st[(i, "q")] = q_sb
-
-        def pp(i):
-            pr = work.tile([P, KP], F32, name="pr", bufs=4)
-            if PENG[i] == "p":
-                nc.vector.tensor_tensor(out=flat(pr[:]), in0=perm(st[(i, "qb")][:]), in1=flat(st[(i, "k")][:]),
-                                        op=ALU.mult)
-            elif PENG[i] == "v":
-                nc.vector.tensor_tensor(out=pr[:], in0=st[(i, "q")][:], in1=st[(i, "k")][:], op=ALU.mult)
-            else:
-                nc.gpsimd.tensor_tensor(out=pr[:], in0=st[(i, "q")][:], in1=st[(i, "k")][:], op=ALU.mult)
-            st[(i, "p")] = pr
-
-        def tkk(i):
-            u, c = divmod(i, C)
-            if c == 0:
-                st[(u, "kkb")] = ps_mid.tile([P, KP], F32, name="bank_mid")
-            turn(st[(u, "kkb")], st[(i, "sq")], c == 0, c == C - 1)
-
-        def ss(i):
-            u, c = divmod(i, C)
-            if SMODE[u] == "F":
-                if c == 0:
-                    st[(u, "s")] = ps_mid.tile([P, KP], F32, name="bank_mid")
-                turn(st[(u, "s")], st[(i, "p")], c == 0, c == C - 1)
-            elif c == 0:
-                st[(u, "s")] = st[(i, "p")]
-            else:
-                s = mid.tile([P, KP], F32, name="s%d" % c)
-                eng = nc.gpsimd if (c == 1 and POOL[u]) else nc.vector
-                eng.tensor_tensor(out=s[:], in0=st[(u, "s")][:], in1=st[(i, "p")][:], op=ALU.add)
-                st[(u, "s")] = s
-
-        def rs(i):
-            u, c = divmod(i, C)
-            if c == C - 1:
-                t = mid.tile([P, KP], F32, name="rs")
-                nc.scalar.activation(out=t[:], in_=st[(u, "kkb")][:], func=ACT.Abs_reciprocal_sqrt,
-                                     bias=EPS / SLOPE)
-                st[(u, "rs")] = t
-
-        def yy(i):
-            u, c = divmod(i, C)
-            if c == C - 1:
-                y = mid.tile([P, KP], F32, name="y")
-                nc.scalar.activation(out=y[:], in_=st[(u, "rs")][:], func=ACT.Square)
-                st[(u, "y")] = y
-
-        def ty(i):
-            u, c = divmod(i, C)
-            if c == C - 1 and SMODE[u] == "M":
-                yb = ps_mid.tile([P, KP], F32, name="bank_mid")
-                turn(yb, st[(u, "y")], True, True)
-                st[(u, "y")] = yb
-
-        def rr(i):
-            u, c = divmod(i, C)
-            if c == C - 1:
-                r = mid.tile([P, KP], F32, name="r")
-                nc.vector.scalar_tensor_tensor(out=r[:], in0=st[(u, "s")][:], scalar=0.0, in1=st[(u, "y")][:],
-                                               op0=ALU.min, op1=ALU.mult)
-                st[(u, "r")] = r
-
-        def tr(i):
-            u, c = divmod(i, C)
-            if c == C - 1 and SMODE[u] == "F":
-                rb = ps_mid.tile([P, KP], F32, name="bank_mid")
-                turn(rb, st[(u, "r")], True, True)
-                st[(u, "r")] = rb
-
-        def tt(i):
-            tk = work.tile([P, KP], F32, name="tk", bufs=3)
-            nc.vector.scalar_tensor_tensor(out=tk[:], in0=st[(i, "k")][:], scalar=-1.0, in1=st[(i // C, "r")][:],
-                                           op0=ALU.mult, op1=ALU.mult)
-            st[(i, "t")] = tk
-
-        def tq(i):
-            db = ps_mx.tile([P, KP], F32, name="bank_mx") if i == 11 else ps_d.tile([P, KP], F32, name="bank_d")
-            turn(db, st[(i, "q")], True, False)
-            st[(i, "d")] = db
-
-        def td(i):
-            turn(st[(i, "d")], st[(i, "t")], False, True)
-
-        def ev(i):
-            j, gi, c = slot(i)
-            h = work.tile([P, KP], BF16, name="h", bufs=3, align_bytes=64)
+                bank = ps_diff.tile([P, KP], F32, name="bank_diff")
+            for u in range(2):
+                nc.tensor.transpose(bank[:, u * P : (u + 1) * P], words[:, u : D // 2 : 2], ident[:])
+            scaled = work.tile([P, D], BF16, name="scaled", align_bytes=64)
             nc.vector.tensor_tensor(
-                out=h[:].rearrange("p (n t) -> p n t", t=PACK),
-                in0=st[(i, "d")][:].rearrange("p (t n) -> p n t", t=PACK),
-                in1=gain[:, gi, :].unsqueeze(1).to_broadcast([P, P, PACK]),
+                out=scaled[:].rearrange("p (n u e) -> p n u e", u=2, e=2),
+                in0=bank[:, 0 : 2 * P].bitcast(BF16).rearrange("p (u n e) -> p n u e", u=2, e=2),
+                in1=x_factor[:].rearrange("p (u e) -> p u e", u=2).unsqueeze(1).to_broadcast([P, P, 2, 2]),
                 op=ALU.mult,
             )
-            st[(i, "h")] = h
+            held["scaled", j, c] = scaled
 
-        def qz(i):
-            codes = work.tile([P, P], U32, name="hc", bufs=12, align_bytes=64)
-            plane = work.tile([P, P], U8, name="hp", bufs=12, align_bytes=64)
-            nc.vector.quantize_mx(out=codes[:].bitcast(FP8X4), scales=plane[:], in_=st[(i, "h")][:])
-            st[(i, "hq")] = (codes, plane)
+        def quantise_x(j, c):
+            codes = keep.tile([P, P], U32, name="x_codes%d%d" % (j, c), align_bytes=64)
+            plane = keep.tile([P, P], U8, name="x_plane%d%d" % (j, c), align_bytes=64)
+            nc.vector.quantize_mx(out=codes[:].bitcast(FP8X4), scales=plane[:], in_=held["scaled", j, c][:])
+            held["x_mx", j, c] = (codes, plane)
 
-        def mo(i):
-            j, gi, c = slot(i)
-            if gi == NG - 1:
-                ob = ps_mx.tile([P, O], F32, name="bank_mx")
-                for a in range(NG):
-                    codes, plane = st[(i - C * (NG - 1 - a), "hq")]
-                    nc.tensor.matmul_mx(out=ob[:], lhsT=codes[:].bitcast(FP8X4), lhsT_scale=plane[:],
-                                        rhs=vw[:, a, :].bitcast(FP4X4), rhs_scale=vs[:, a * O : (a + 1) * O],
-                                        start=(a == 0), stop=(a == NG - 1))
-                st[(i, "ob")] = ob
 
-        def mpass(i, a):
-            codes, plane = st[(i - C * (NG - 1 - a), "hq")]
-            nc.tensor.matmul_mx(out=st[(i, "ob")][:], lhsT=codes[:].bitcast(FP8X4), lhsT_scale=plane[:],
-                                rhs=vw[:, a, :].bitcast(FP4X4), rhs_scale=vs[:, a * O : (a + 1) * O],
-                                start=(a == 0), stop=(a == NG - 1))
+        def project(unit, c, words, plane):
+            j, half = divmod(unit, HALVES)
+            x_codes, x_plane = held["x_mx", j, c]
+            bank = ps_mx.tile([P, KP], F32, name="bank_mx")
+            nc.tensor.matmul_mx(
+                out=bank[:], lhsT=x_codes[:].bitcast(FP8X4), lhsT_scale=x_plane[:],
+                rhs=words[half][:].bitcast(FP4X4), rhs_scale=plane[:, half * KP : (half + 1) * KP],
+                start=True, stop=True,
+            )
+            return bank
 
-        def m1(i):
-            st[(i, "ob")] = ps_mx.tile([P, O], F32, name="bank_mx")
-            mpass(i, 0)
+        def matmul_k(unit, c):
+            held["k_bank", unit, c] = project(unit, c, u_tiles, u_plane)
 
-        def m2(i):
-            mpass(i, 1)
+        def matmul_q(unit, c):
+            held["q_bank", unit, c] = project(unit, c, w_tiles, w_plane)
 
-        def oc(i):
-            j, gi, c = slot(i)
-            if gi == NG - 1:
-                res = work.tile([P, O], F32, name="res", bufs=3)
-                copy_on(OENG[j * C + c], res[:], st[(i, "ob")][:])
-                nc.sync.dma_start(out=out[c, j * P : (j + 1) * P, :], in_=res[:])
+        def copy_k(unit, c, on_vector=False):
+            if c == 0:
+                held["k_all", unit] = work.tile([P, C * KP], F32, name="k_all", bufs=3)
+            k_c = held["k_all", unit][:, c * KP : (c + 1) * KP]
+            copy(on_vector, as_reordered(k_c), as_stored(held["k_bank", unit, c][:]))
+            held["k", unit, c] = k_c
 
-        def x1(i):
-            if i < C:
-                turn_x(1, i)
+        def square_k(unit, c):
+            k_sq = work.tile([P, KP], F32, name="k_sq", bufs=C)
+            nc.scalar.activation(
+                out=as_reordered(k_sq[:]), in_=as_stored(held["k_bank", unit, c][:]), func=ACT.Square,
+                scale=(1.0 / SLOPE) ** 0.5,
+            )
+            held["k_sq", unit, c] = k_sq
 
-        def x1q(i):
-            if i < C:
-                quant_x(1, i)
+        def copy_q(unit, c):
+            q_c = work.tile([P, KP], F32, name="q_c", bufs=10)
+            nc.scalar.copy(out=as_reordered(q_c[:]), in_=as_stored(held["q_bank", unit, c][:]))
+            held["q", unit, c] = q_c
 
-        stages = dict(mk=mk, mq=mq, kc=kc, sq=sq, qc=qc, pp=pp, tkk=tkk, ss=ss, rs=rs, yy=yy, ty=ty, rr=rr, tr=tr,
-                      tt=tt, tq=tq, td=td, ev=ev, qz=qz, mo=mo, oc=oc, x1=x1, x1q=x1q, m1=m1, m2=m2)
-        with ExitStack() as sched:
-            if MANUAL:
-                sched.enter_context(tc.manual_schedule())
-            spin(5)
+        def product_qk(unit, c):
+            qk = work.tile([P, KP], F32, name="qk", bufs=C + 1)
+            nc.vector.tensor_tensor(
+                out=as_reordered(qk[:]), in0=as_stored(held["q_bank", unit, c][:]),
+                in1=as_reordered(held["k", unit, c][:]), op=ALU.mult,
+            )
+            held["qk", unit, c] = qk
+
+        def first_add_s(unit):
+            part = mid.tile([P, KP], F32, name="s_part")
+            nc.gpsimd.tensor_tensor(out=part[:], in0=held["qk", unit, 0][:], in1=held["qk", unit, 1][:], op=ALU.add)
+            held["s_part", unit] = part
+
+        def second_add_s(unit):
+            s = mid.tile([P, KP], F32, name="s")
+            nc.vector.tensor_tensor(out=s[:], in0=held["s_part", unit][:], in1=held["qk", unit, 2][:], op=ALU.add)
+            held["s", unit] = s
+
+        def add_kk(unit, c):
+            if c == 0:
+                held["kk_bank", unit] = ps_kk.tile([P, KP], F32, name="bank_kk")
+            turn(held["kk_bank", unit], held["k_sq", unit, c], c == 0, c == C - 1)
+
+        def inverse_root(unit):
+            root = mid.tile([P, KP], F32, name="root")
+            nc.scalar.activation(
+                out=root[:], in_=held["kk_bank", unit][:], func=ACT.Abs_reciprocal_sqrt, bias=EPS / SLOPE
+            )
+            held["root", unit] = root
+
+        def reciprocal(unit):
+            recip = mid.tile([P, KP], F32, name="recip")
+            nc.scalar.activation(out=recip[:], in_=held["root", unit][:], func=ACT.Square)
+            held["recip", unit] = recip
+
+        def turn_reciprocal(unit):
+            bank = ps_kk.tile([P, KP], F32, name="bank_kk")
+            turn(bank, held["recip", unit], True, True)
+            held["recip_bank", unit] = bank
+
+        def coefficient(unit):
+            r = mid.tile([P, KP], F32, name="r")
+            nc.vector.scalar_tensor_tensor(
+                out=r[:], in0=held["s", unit][:], scalar=0.0, in1=held["recip_bank", unit][:],
+                op0=ALU.min, op1=ALU.mult,
+            )
+            held["r", unit] = r
+
+        def removed(unit, c):
+            rk = work.tile([P, KP], F32, name="rk", bufs=C)
+            nc.vector.scalar_tensor_tensor(
+                out=rk[:], in0=held["k", unit, c][:], scalar=-1.0, in1=held["r", unit][:],
+                op0=ALU.mult, op1=ALU.mult,
+            )
+            held["rk", unit, c] = rk
+
+        def removed_pair(unit):
+            rk = work.tile([P, 2 * KP], F32, name="rk_pair", bufs=2)
+            nc.vector.scalar_tensor_tensor(
+                out=rk[:].rearrange("n (c f) -> n c f", c=2),
+                in0=held["k_all", unit][:, KP : C * KP].rearrange("n (c f) -> n c f", c=2), scalar=-1.0,
+                in1=held["r", unit][:].unsqueeze(1).to_broadcast([P, 2, KP]), op0=ALU.mult, op1=ALU.mult,
+            )
+            held["rk", unit, 1] = rk[:, 0:KP]
+            held["rk", unit, 2] = rk[:, KP : 2 * KP]
+
+        def turn_q(unit, c, spare_bank=False):
+            if spare_bank:
+                bank = ps_mx.tile([P, KP], F32, name="bank_mx")
+            else:
+                bank = ps_diff.tile([P, KP], F32, name="bank_diff")
+            turn(bank, held["q", unit, c], True, False)
+            held["diff_bank", unit, c] = bank
+
+        def turn_removed(unit, c):
+            turn(held["diff_bank", unit, c], held["rk", unit, c], False, True)
+
+        def apply_gain(unit, c):
+            if c == 0:
+                held["h_all", unit] = work.tile([P, C * KP], BF16, name="h_all", bufs=2, align_bytes=64)
+            h_c = held["h_all", unit][:, c * KP : (c + 1) * KP]
+            nc.vector.tensor_tensor(
+                out=h_c.rearrange("p (n t) -> p n t", t=PACK),
+                in0=held["diff_bank", unit, c][:].rearrange("p (t n) -> p n t", t=PACK),
+                in1=gain[:, unit % HALVES, :].unsqueeze(1).to_broadcast([P, P, PACK]),
+                op=ALU.mult,
+            )
+            held["h", unit, c] = h_c
+
+        def quantise_h(unit, c):
+            codes = work.tile([P, P], U32, name="h_codes", bufs=C * UNITS, align_bytes=64)
+            plane = work.tile([P, P], U8, name="h_plane", bufs=C * UNITS, align_bytes=64)
+            nc.vector.quantize_mx(out=codes[:].bitcast(FP8X4), scales=plane[:], in_=held["h", unit, c][:])
+            held["h_mx", unit, c] = (codes, plane)
+
+        def quantise_h_pair(unit):
+            codes = work.tile([P, 2 * P], U32, name="h_codes_pair", bufs=LAST, align_bytes=64)
+            plane = work.tile([P, 2 * P], U8, name="h_plane_pair", bufs=LAST, align_bytes=64)
+            nc.vector.quantize_mx(
+                out=codes[:].bitcast(FP8X4), scales=plane[:], in_=held["h_all", unit][:, 0 : 2 * KP]
+            )
+            for c in range(2):
+                held["h_mx", unit, c] = (codes[:, c * P : (c + 1) * P], plane[:, c * P : (c + 1) * P])
+
+        def output_pass(j, c, half):
+            if half == 0:
+                held["out_bank", j, c] = ps_mx.tile([P, O], F32, name="bank_mx")
+            h_codes, h_plane = held["h_mx", j * HALVES + half, c]
+            nc.tensor.matmul_mx(
+                out=held["out_bank", j, c][:], lhsT=h_codes[:].bitcast(FP8X4), lhsT_scale=h_plane[:],
+                rhs=v_tile[:, half, :].bitcast(FP4X4), rhs_scale=v_plane[:, half * O : (half + 1) * O],
+                start=(half == 0), stop=(half == HALVES - 1),
+            )
+
+        def output(j, c):
+            for half in range(HALVES):
+                output_pass(j, c, half)
+
+        def store(j, c, on_vector=False):
+            result = work.tile([P, O], F32, name="result", bufs=C)
+            copy(on_vector, result[:], held["out_bank", j, c][:])
+            nc.sync.dma_start(out=out[c, j * P : (j + 1) * P, :], in_=result[:])
+
+        ctx.enter_context(tc.manual_schedule())
+
+        for c in range(C):
+            widen_x(0, c, on_vector=(c != 1))
+        for c in range(C):
+            widen_x(1, c, on_vector=False)
+        for c in range(C):
+            turn_x(0, c)
+            if c > 0:
+                quantise_x(0, c - 1)
+        quantise_x(0, C - 1)
+        turn_x(1, 0)
+        for c in range(C):
+            matmul_k(0, c)
+        matmul_q(0, 0)
+        matmul_q(0, 1)
+        square_k(0, 0)
+        copy_k(0, 0, on_vector=True)
+        square_k(0, 1)
+        quantise_x(1, 0)
+        copy_k(0, 1)
+        square_k(0, 2)
+        add_kk(0, 0)
+        add_kk(0, 1)
+        product_qk(0, 0)
+        product_qk(0, 1)
+        first_add_s(0)
+        turn_x(1, 1)
+        add_kk(0, 2)
+        turn_x(1, 2)
+        matmul_q(0, 2)
+        copy_k(0, 2)
+        inverse_root(0)
+        reciprocal(0)
+        copy_q(0, 0)
+        product_qk(0, 2)
+        matmul_k(1, 0)
+        matmul_k(1, 1)
+        turn_reciprocal(0)
+        copy_q(0, 1)
+        second_add_s(0)
+        quantise_x(1, 1)
+        matmul_k(1, 2)
+        copy_q(0, 2)
+        turn_q(0, 0)
+        turn_q(0, 1)
+        square_k(1, 0)
+
+        for cur in range(LAST):
+            nxt = cur + 1
+            last_round = nxt == LAST
+            coefficient(cur)
+            copy_k(nxt, 0)
             for c in range(C):
-                widen(0, c, WENG[c])
-            for c in range(C):
-                widen(1, c, "s")
-            for c in range(C):
-                turn_x(0, c)
-                if c > 0:
-                    quant_x(0, c - 1)
-            quant_x(0, C - 1)
-            spin(1)
-            units = NT * NG
-            for name, c in HEAD:
-                stages[name](c)
-            for u in range(units - 1):
-                for name, du, c in PERIOD:
-                    if 0 <= u - du < units:
-                        stages[name](C * (u - du) + c)
-            for name, i in TAIL:
-                stages[name](i)
+                matmul_q(nxt, c)
+            if cur == 0:
+                quantise_x(1, C - 1)
+            else:
+                quantise_h(cur - 1, C - 1)
+            removed(cur, 0)
+            square_k(nxt, 1)
+            add_kk(nxt, 0)
+            removed_pair(cur)
+            copy_k(nxt, 1)
+            add_kk(nxt, 1)
+            turn_removed(cur, 0)
+            square_k(nxt, 2)
+            product_qk(nxt, 0)
+            copy_k(nxt, 2)
+            add_kk(nxt, 2)
+            turn_removed(cur, 1)
+            product_qk(nxt, 1)
+            first_add_s(nxt)
+            copy_q(nxt, 0)
+            apply_gain(cur, 0)
+            inverse_root(nxt)
+            turn_q(cur, 2)
+            turn_removed(cur, 2)
+            if last_round:
+                output(0, 0)
+            else:
+                for c in range(C):
+                    matmul_k(nxt + 1, c)
+            product_qk(nxt, 2)
+            copy_q(nxt, 1)
+            apply_gain(cur, 1)
+            reciprocal(nxt)
+            turn_reciprocal(nxt)
+            if last_round:
+                output(0, 1)
+                output(0, 2)
+            apply_gain(cur, 2)
+            copy_q(nxt, 2)
+            second_add_s(nxt)
+            turn_q(nxt, 0)
+            turn_q(nxt, 1)
+            quantise_h_pair(cur)
+            if last_round:
+                for c in range(C):
+                    store(0, c)
+            else:
+                square_k(nxt + 1, 0)
+
+        coefficient(LAST)
+        quantise_h(LAST - 1, C - 1)
+        removed(LAST, 0)
+        removed(LAST, 1)
+        turn_removed(LAST, 0)
+        turn_q(LAST, 2, spare_bank=True)
+        removed(LAST, 2)
+        turn_removed(LAST, 1)
+        apply_gain(LAST, 0)
+        turn_removed(LAST, 2)
+        for c in range(C):
+            output_pass(1, c, 0)
+        apply_gain(LAST, 1)
+        for c in range(2):
+            quantise_h(LAST, c)
+            output_pass(1, c, 1)
+        apply_gain(LAST, 2)
+        store(1, 0)
+        quantise_h(LAST, 2)
+        output_pass(1, 2, 1)
+        store(1, 1)
+        store(1, 2, on_vector=True)

from contextlib import ExitStack

import concourse.mybir as mybir
from concourse.masks import make_identity

F32 = mybir.dt.float32
BF16 = mybir.dt.bfloat16
I32 = mybir.dt.int32
U32 = mybir.dt.uint32
U8 = mybir.dt.uint8
FP8 = mybir.dt.float8_e4m3fn
FP8X4 = mybir.dt.float8_e4m3fn_x4
FP4X4 = mybir.dt.float4_e2m1fn_x4
ALU = mybir.AluOpType
ACT = mybir.ActivationFunctionType

C, N, D, F, O = 3, 256, 512, 1024, 512
P = 128
PACK = 4
KP = P * PACK
HALVES = F // KP
UNITS = (N // P) * HALVES
LAST = UNITS - 1
SLOPE = 0.8
EPS = 1e-4

BANKS_MX, BANKS_KK, BANKS_DIFF = 5, 1, 2

FLOPS = 2 * C * N * D * F * 2 + 2 * C * N * F * O


def tile_vectorneurondirectionalleaky_w4_kernel(
    tc, x_bytes, x_scale, w_words, w_scales, u_words, u_scales, g, v_words, v_scales, out
):
    nc = tc.nc
    with ExitStack() as ctx:
        keep = ctx.enter_context(tc.tile_pool(name="keep", bufs=1))
        work = ctx.enter_context(tc.tile_pool(name="work", bufs=2 * C))
        mid = ctx.enter_context(tc.tile_pool(name="mid", bufs=2))
        ps_mx = ctx.enter_context(tc.psum_pool(name="ps_mx", bufs=BANKS_MX))
        ps_kk = ctx.enter_context(tc.psum_pool(name="ps_kk", bufs=BANKS_KK))
        ps_diff = ctx.enter_context(tc.psum_pool(name="ps_diff", bufs=BANKS_DIFF))

        u_plane = keep.tile([P, F], U8, name="u_plane", align_bytes=64)
        w_plane = keep.tile([P, F], U8, name="w_plane", align_bytes=64)
        v_plane = keep.tile([P, HALVES * O], U8, name="v_plane", align_bytes=64)
        warm = keep.tile([P, 8], F32, name="warm")
        nc.vector.memset(u_plane[:].bitcast(I32), 0)
        nc.vector.memset(w_plane[:].bitcast(I32), 0)
        nc.vector.memset(warm[:, 0:1], 1.0)
        nc.vector.memset(v_plane[:].bitcast(I32), 0)
        nc.scalar.activation(out=warm[:, 4:5], in_=warm[:, 0:1], func=ACT.Abs_reciprocal_sqrt)

        ident = keep.tile([P, P], F32, name="ident")
        make_identity(nc, ident[:])

        def load_plane(plane, rows):
            for quad in range(4):
                nc.sync.dma_start(
                    out=plane[32 * quad : 32 * quad + 4, :].bitcast(I32),
                    in_=rows[4 * quad : 4 * quad + 4, :].bitcast(I32),
                )

        def load_words(name, words, half):
            tile = keep.tile([P, 2 * KP], U8, name=name, align_bytes=64)
            nc.sync.dma_start(
                out=tile[:].bitcast(I32), in_=words[0, :, 2 * KP * half : 2 * KP * (half + 1)].bitcast(I32)
            )
            return tile

        def load_x(j):
            tile = keep.tile([P, C, D], U8, name="x_raw%d" % j, align_bytes=64)
            nc.sync.dma_start(out=tile[:], in_=x_bytes[:, j * P : (j + 1) * P, :].rearrange("c n k -> n c k"))
            return tile

        x_raw = {}
        u_tiles = {}
        w_tiles = {}
        x_raw[0] = load_x(0)
        x_factor = keep.tile([P, PACK], F32, name="x_factor")
        nc.sync.dma_start(out=x_factor[:], in_=x_scale.rearrange("a b (p t) -> p (a b t)", t=PACK))
        u_tiles[0] = load_words("u_words0", u_words, 0)
        load_plane(u_plane, u_scales[0])
        x_raw[1] = load_x(1)
        w_tiles[0] = load_words("w_words0", w_words, 0)
        load_plane(w_plane, w_scales[0])
        u_tiles[1] = load_words("u_words1", u_words, 1)
        w_tiles[1] = load_words("w_words1", w_words, 1)
        gain = keep.tile([P, HALVES, PACK], BF16, name="gain")
        nc.sync.dma_start(out=gain[:], in_=g.rearrange("(a p t) -> p a t", p=P, t=PACK))
        v_tile = keep.tile([P, HALVES, 2 * O], U8, name="v_tile", align_bytes=64)
        nc.sync.dma_start(out=v_tile[:].bitcast(I32), in_=v_words.rearrange("a p b -> p a b").bitcast(I32))
        for quad in range(4):
            nc.sync.dma_start(
                out=v_plane[32 * quad : 32 * quad + 4, :].bitcast(I32).rearrange("r (a n) -> r a n", a=HALVES),
                in_=v_scales[:, 4 * quad : 4 * quad + 4, :].bitcast(I32).rearrange("a r n -> r a n"),
            )

        held = {}

        def copy(on_vector, dst, src):
            if on_vector:
                nc.vector.tensor_copy(out=dst, in_=src)
            else:
                nc.scalar.copy(out=dst, in_=src)

        def as_stored(bank):
            return bank.rearrange("n (m t) -> n t m", t=PACK)

        def as_reordered(tile):
            return tile.rearrange("n (t m) -> n t m", t=PACK)

        def turn(bank, src, start, stop):
            for t in range(PACK):
                cols = slice(t * P, (t + 1) * P)
                nc.tensor.matmul(
                    bank[:, cols], lhsT=src[:, cols], rhs=ident[:], is_transpose=True,
                    start=(start and t == 0), stop=(stop and t == PACK - 1),
                )


        def widen_x(j, c, on_vector):
            wide = work.tile([P, D], BF16, name="wide", align_bytes=64)
            copy(on_vector, wide[:], x_raw[j][:, c, :].bitcast(FP8))
            held["wide", j, c] = wide

        def turn_x(j, c):
            words = held["wide", j, c][:].bitcast(F32)
            if j == 0:
                bank = ps_mx.tile([P, KP], F32, name="bank_mx")
            else:
                bank = ps_diff.tile([P, KP], F32, name="bank_diff")
            for u in range(2):
                nc.tensor.transpose(bank[:, u * P : (u + 1) * P], words[:, u : D // 2 : 2], ident[:])
            scaled = work.tile([P, D], BF16, name="scaled", align_bytes=64)
            nc.vector.tensor_tensor(
                out=scaled[:].rearrange("p (n u e) -> p n u e", u=2, e=2),
                in0=bank[:, 0 : 2 * P].bitcast(BF16).rearrange("p (u n e) -> p n u e", u=2, e=2),
                in1=x_factor[:].rearrange("p (u e) -> p u e", u=2).unsqueeze(1).to_broadcast([P, P, 2, 2]),
                op=ALU.mult,
            )
            held["scaled", j, c] = scaled

        def quantise_x(j, c):
            codes = keep.tile([P, P], U32, name="x_codes%d%d" % (j, c), align_bytes=64)
            plane = keep.tile([P, P], U8, name="x_plane%d%d" % (j, c), align_bytes=64)
            nc.vector.quantize_mx(out=codes[:].bitcast(FP8X4), scales=plane[:], in_=held["scaled", j, c][:])
            held["x_mx", j, c] = (codes, plane)


        def project(unit, c, words, plane):
            j, half = divmod(unit, HALVES)
            x_codes, x_plane = held["x_mx", j, c]
            bank = ps_mx.tile([P, KP], F32, name="bank_mx")
            nc.tensor.matmul_mx(
                out=bank[:], lhsT=x_codes[:].bitcast(FP8X4), lhsT_scale=x_plane[:],
                rhs=words[half][:].bitcast(FP4X4), rhs_scale=plane[:, half * KP : (half + 1) * KP],
                start=True, stop=True,
            )
            return bank

        def matmul_k(unit, c):
            held["k_bank", unit, c] = project(unit, c, u_tiles, u_plane)

        def matmul_q(unit, c):
            held["q_bank", unit, c] = project(unit, c, w_tiles, w_plane)

        def copy_k(unit, c, on_vector=False):
            if c == 0:
                held["k_all", unit] = work.tile([P, C * KP], F32, name="k_all", bufs=3)
            k_c = held["k_all", unit][:, c * KP : (c + 1) * KP]
            copy(on_vector, as_reordered(k_c), as_stored(held["k_bank", unit, c][:]))
            held["k", unit, c] = k_c

        def square_k(unit, c):
            k_sq = work.tile([P, KP], F32, name="k_sq", bufs=C)
            nc.scalar.activation(
                out=as_reordered(k_sq[:]), in_=as_stored(held["k_bank", unit, c][:]), func=ACT.Square,
                scale=(1.0 / SLOPE) ** 0.5,
            )
            held["k_sq", unit, c] = k_sq

        def copy_q(unit, c):
            q_c = work.tile([P, KP], F32, name="q_c", bufs=10)
            nc.scalar.copy(out=as_reordered(q_c[:]), in_=as_stored(held["q_bank", unit, c][:]))
            held["q", unit, c] = q_c

        def product_qk(unit, c):
            qk = work.tile([P, KP], F32, name="qk", bufs=C + 1)
            nc.vector.tensor_tensor(
                out=as_reordered(qk[:]), in0=as_stored(held["q_bank", unit, c][:]),
                in1=as_reordered(held["k", unit, c][:]), op=ALU.mult,
            )
            held["qk", unit, c] = qk

        def first_add_s(unit):
            part = mid.tile([P, KP], F32, name="s_part")
            nc.gpsimd.tensor_tensor(out=part[:], in0=held["qk", unit, 0][:], in1=held["qk", unit, 1][:], op=ALU.add)
            held["s_part", unit] = part

        def second_add_s(unit):
            s = mid.tile([P, KP], F32, name="s")
            nc.vector.tensor_tensor(out=s[:], in0=held["s_part", unit][:], in1=held["qk", unit, 2][:], op=ALU.add)
            held["s", unit] = s

        def add_kk(unit, c):
            if c == 0:
                held["kk_bank", unit] = ps_kk.tile([P, KP], F32, name="bank_kk")
            turn(held["kk_bank", unit], held["k_sq", unit, c], c == 0, c == C - 1)

        def inverse_root(unit):
            root = mid.tile([P, KP], F32, name="root")
            nc.scalar.activation(
                out=root[:], in_=held["kk_bank", unit][:], func=ACT.Abs_reciprocal_sqrt, bias=EPS / SLOPE
            )
            held["root", unit] = root

        def reciprocal(unit):
            recip = mid.tile([P, KP], F32, name="recip")
            nc.scalar.activation(out=recip[:], in_=held["root", unit][:], func=ACT.Square)
            held["recip", unit] = recip

        def turn_reciprocal(unit):
            bank = ps_kk.tile([P, KP], F32, name="bank_kk")
            turn(bank, held["recip", unit], True, True)
            held["recip_bank", unit] = bank

        def coefficient(unit):
            r = mid.tile([P, KP], F32, name="r")
            nc.vector.scalar_tensor_tensor(
                out=r[:], in0=held["s", unit][:], scalar=0.0, in1=held["recip_bank", unit][:],
                op0=ALU.min, op1=ALU.mult,
            )
            held["r", unit] = r

        def removed(unit, c):
            rk = work.tile([P, KP], F32, name="rk", bufs=C)
            nc.vector.scalar_tensor_tensor(
                out=rk[:], in0=held["k", unit, c][:], scalar=-1.0, in1=held["r", unit][:],
                op0=ALU.mult, op1=ALU.mult,
            )
            held["rk", unit, c] = rk

        def removed_pair(unit):
            rk = work.tile([P, 2 * KP], F32, name="rk_pair", bufs=2)
            nc.vector.scalar_tensor_tensor(
                out=rk[:].rearrange("n (c f) -> n c f", c=2),
                in0=held["k_all", unit][:, KP : C * KP].rearrange("n (c f) -> n c f", c=2), scalar=-1.0,
                in1=held["r", unit][:].unsqueeze(1).to_broadcast([P, 2, KP]), op0=ALU.mult, op1=ALU.mult,
            )
            held["rk", unit, 1] = rk[:, 0:KP]
            held["rk", unit, 2] = rk[:, KP : 2 * KP]

        def turn_q(unit, c, spare_bank=False):
            if spare_bank:
                bank = ps_mx.tile([P, KP], F32, name="bank_mx")
            else:
                bank = ps_diff.tile([P, KP], F32, name="bank_diff")
            turn(bank, held["q", unit, c], True, False)
            held["diff_bank", unit, c] = bank

        def turn_removed(unit, c):
            turn(held["diff_bank", unit, c], held["rk", unit, c], False, True)

        def apply_gain(unit, c):
            if c == 0:
                held["h_all", unit] = work.tile([P, C * KP], BF16, name="h_all", bufs=2, align_bytes=64)
            h_c = held["h_all", unit][:, c * KP : (c + 1) * KP]
            nc.vector.tensor_tensor(
                out=h_c.rearrange("p (n t) -> p n t", t=PACK),
                in0=held["diff_bank", unit, c][:].rearrange("p (t n) -> p n t", t=PACK),
                in1=gain[:, unit % HALVES, :].unsqueeze(1).to_broadcast([P, P, PACK]),
                op=ALU.mult,
            )
            held["h", unit, c] = h_c

        def quantise_h(unit, c):
            codes = work.tile([P, P], U32, name="h_codes", bufs=C * UNITS, align_bytes=64)
            plane = work.tile([P, P], U8, name="h_plane", bufs=C * UNITS, align_bytes=64)
            nc.vector.quantize_mx(out=codes[:].bitcast(FP8X4), scales=plane[:], in_=held["h", unit, c][:])
            held["h_mx", unit, c] = (codes, plane)

        def quantise_h_pair(unit):
            codes = work.tile([P, 2 * P], U32, name="h_codes_pair", bufs=LAST, align_bytes=64)
            plane = work.tile([P, 2 * P], U8, name="h_plane_pair", bufs=LAST, align_bytes=64)
            nc.vector.quantize_mx(
                out=codes[:].bitcast(FP8X4), scales=plane[:], in_=held["h_all", unit][:, 0 : 2 * KP]
            )
            for c in range(2):
                held["h_mx", unit, c] = (codes[:, c * P : (c + 1) * P], plane[:, c * P : (c + 1) * P])

        def output_pass(j, c, half):
            if half == 0:
                held["out_bank", j, c] = ps_mx.tile([P, O], F32, name="bank_mx")
            h_codes, h_plane = held["h_mx", j * HALVES + half, c]
            nc.tensor.matmul_mx(
                out=held["out_bank", j, c][:], lhsT=h_codes[:].bitcast(FP8X4), lhsT_scale=h_plane[:],
                rhs=v_tile[:, half, :].bitcast(FP4X4), rhs_scale=v_plane[:, half * O : (half + 1) * O],
                start=(half == 0), stop=(half == HALVES - 1),
            )

        def output(j, c):
            for half in range(HALVES):
                output_pass(j, c, half)

        def store(j, c, on_vector=False):
            result = work.tile([P, O], F32, name="result", bufs=C)
            copy(on_vector, result[:], held["out_bank", j, c][:])
            nc.sync.dma_start(out=out[c, j * P : (j + 1) * P, :], in_=result[:])

        ctx.enter_context(tc.manual_schedule())

        for c in range(C):
            widen_x(0, c, on_vector=(c != 1))
        for c in range(C):
            widen_x(1, c, on_vector=False)
        for c in range(C):
            turn_x(0, c)
            if c > 0:
                quantise_x(0, c - 1)
        quantise_x(0, C - 1)
        turn_x(1, 0)
        for c in range(C):
            matmul_k(0, c)
        matmul_q(0, 0)
        matmul_q(0, 1)
        square_k(0, 0)
        copy_k(0, 0, on_vector=True)
        square_k(0, 1)
        quantise_x(1, 0)
        copy_k(0, 1)
        square_k(0, 2)
        add_kk(0, 0)
        add_kk(0, 1)
        product_qk(0, 0)
        product_qk(0, 1)
        first_add_s(0)
        turn_x(1, 1)
        add_kk(0, 2)
        turn_x(1, 2)
        matmul_q(0, 2)
        copy_k(0, 2)
        inverse_root(0)
        reciprocal(0)
        copy_q(0, 0)
        product_qk(0, 2)
        matmul_k(1, 0)
        matmul_k(1, 1)
        turn_reciprocal(0)
        copy_q(0, 1)
        second_add_s(0)
        quantise_x(1, 1)
        matmul_k(1, 2)
        copy_q(0, 2)
        turn_q(0, 0)
        turn_q(0, 1)
        square_k(1, 0)

        for cur in range(LAST):
            nxt = cur + 1
            last_round = nxt == LAST
            coefficient(cur)
            copy_k(nxt, 0)
            for c in range(C):
                matmul_q(nxt, c)
            if cur == 0:
                quantise_x(1, C - 1)
            else:
                quantise_h(cur - 1, C - 1)
            removed(cur, 0)
            square_k(nxt, 1)
            add_kk(nxt, 0)
            removed_pair(cur)
            copy_k(nxt, 1)
            add_kk(nxt, 1)
            turn_removed(cur, 0)
            square_k(nxt, 2)
            product_qk(nxt, 0)
            copy_k(nxt, 2)
            add_kk(nxt, 2)
            turn_removed(cur, 1)
            product_qk(nxt, 1)
            first_add_s(nxt)
            copy_q(nxt, 0)
            apply_gain(cur, 0)
            inverse_root(nxt)
            turn_q(cur, 2)
            turn_removed(cur, 2)
            if last_round:
                output(0, 0)
            else:
                for c in range(C):
                    matmul_k(nxt + 1, c)
            product_qk(nxt, 2)
            copy_q(nxt, 1)
            apply_gain(cur, 1)
            reciprocal(nxt)
            turn_reciprocal(nxt)
            if last_round:
                output(0, 1)
                output(0, 2)
            apply_gain(cur, 2)
            copy_q(nxt, 2)
            second_add_s(nxt)
            turn_q(nxt, 0)
            turn_q(nxt, 1)
            quantise_h_pair(cur)
            if last_round:
                for c in range(C):
                    store(0, c)
            else:
                square_k(nxt + 1, 0)

        coefficient(LAST)
        quantise_h(LAST - 1, C - 1)
        removed(LAST, 0)
        removed(LAST, 1)
        turn_removed(LAST, 0)
        turn_q(LAST, 2, spare_bank=True)
        removed(LAST, 2)
        turn_removed(LAST, 1)
        apply_gain(LAST, 0)
        turn_removed(LAST, 2)
        for c in range(C):
            output_pass(1, c, 0)
        apply_gain(LAST, 1)
        for c in range(2):
            quantise_h(LAST, c)
            output_pass(1, c, 1)
        apply_gain(LAST, 2)
        store(1, 0)
        quantise_h(LAST, 2)
        output_pass(1, 2, 1)
        store(1, 1)
        store(1, 2, on_vector=True)
